import numpy as np
import ml_dtypes


def mxq(x, axis, fmt="e4m3"):
    dtype, down = {"e4m3": (ml_dtypes.float8_e4m3fn, 7), "e5m2": (ml_dtypes.float8_e5m2, 14)}[fmt]
    v = np.moveaxis(np.asarray(x, np.float32).astype(ml_dtypes.bfloat16).astype(np.float64), axis, -1)
    blocks = v.reshape(v.shape[:-1] + (-1, 32))
    amax = np.abs(blocks).max(-1, keepdims=True)
    byte = np.maximum(np.where(amax > 0, np.frexp(amax)[1] - 1 + 127, 0) - down, 1)
    scale = np.exp2(byte - 127.0)
    codes = (blocks / scale).astype(np.float32).astype(dtype).astype(np.float64)
    return np.moveaxis((codes * scale).reshape(v.shape), -1, axis)


WIDE = False


def mx_kscale(k):
    if not WIDE:
        return np.ones(k)
    levels = np.array([10, -10, 5, -5, 0])
    if k % 512:
        return np.exp2(np.random.permutation(np.resize(levels, k // 32))).repeat(32)
    a = np.empty((k // 512, 16))
    for p in range(k // 512):
        a[p, :8] = np.random.permutation(np.resize(levels, 8))
        for g in range(8):
            far = levels[np.abs(levels - a[p, g]) >= 10]
            a[p, g + 8] = far[np.random.randint(len(far))]
    return np.exp2(a.ravel()).repeat(32)


def f64(x):
    return np.asarray(x).astype(np.float64)


def striped(idx):
    return np.tile(idx.reshape(-1, 16).T, (8, 1)).astype(np.uint16)


def unstriped(offs):
    return offs[:16].T.reshape(-1).astype(np.int64)


def striped8(idx):
    return np.concatenate([x.reshape(-1, 16).T for x in idx]).astype(np.uint16)


def runs(offs, k):
    lists = np.stack([offs[16 * r : 16 * r + 16].T.reshape(-1) for r in range(8)]).astype(np.int64)
    return lists[np.arange(k) % 512 // 64]


def pack_weight(w):
    k, n = w.shape
    w = f64(np.asarray(w, np.float32).astype(ml_dtypes.bfloat16)).reshape(k // 32, 32, n)
    amax = np.abs(w).max(1)
    byte = np.clip(np.where(amax > 0, np.frexp(amax)[1] - 1 + 127 - 7, 1), 1, 254)
    scaled = (w * np.exp2(127.0 - byte)[:, None, :]).reshape(k, n).astype(np.float32)
    words = np.ascontiguousarray(scaled.reshape(k // 512, 128, 4, n).transpose(0, 1, 3, 2)).astype(ml_dtypes.float8_e4m3fn).view(np.uint8)
    return words, np.ascontiguousarray(byte.astype(np.uint8).reshape(k // 512, 16, n))


def unpack_weight(words, scales):
    g, p, n, _ = words.shape
    vals = np.ascontiguousarray(words).view(ml_dtypes.float8_e4m3fn).astype(np.float64) * np.repeat(np.exp2(scales.astype(np.float64) - 127.0), 8, axis=1)[..., None]
    return vals.transpose(0, 1, 3, 2).reshape(g * 512, n)


def relu(v):
    return np.maximum(v, 0.0)


def sigmoid(v):
    return 1.0 / (1.0 + np.exp(-np.maximum(v, -700.0)))


K, T, S, G, H, C = 512, 1024, 256, 2048, 512, 512


def setup_inputs():
    n = np.random.standard_normal
    s = mx_kscale(K)[:, None]
    packed_xT = pack_weight(n((K, T)) * s)
    packed_dT = pack_weight(n((K, G)) / s)
    return {
        "x_words": packed_xT[0],
        "x_scales": packed_xT[1],
        "d_words": packed_dT[0],
        "d_scales": packed_dT[1],
        "gs": (np.random.uniform(0.5, 1.5, (K, 1)) / s).astype(np.float32),
        "offs": striped(np.random.permutation(T)[:S]),
        "k1": striped8(np.random.randint(0, G, (8, H))),
        "n1": striped(np.random.permutation(S)),
        "cand": striped(np.random.permutation(T)[:C]),
        "two": striped(np.random.permutation(T)[:S]),
        "k2": striped8(np.random.randint(0, G, (8, H))),
        "n2": striped(np.random.permutation(S)),
        "n3": striped(np.random.permutation(S)),
    }


def reference(x_words, x_scales, d_words, d_scales, gs, offs, k1, n1, cand, two, k2, n2, n3):
    x_cand = unpack_weight(x_words, x_scales)[:, unstriped(cand)]
    d_k1 = unpack_weight(d_words, d_scales)[np.arange(K)[:, None], runs(k1, K)]
    xq = unpack_weight(x_words, x_scales)[:, unstriped(offs)]
    h = 0.0625 * (d_k1.T @ xq)
    rl = relu(h)
    ds = np.zeros((H, S))
    ds[:, unstriped(n1)] = rl
    z = f64(gs) * (ds - (0.5 * h))
    a = 0.0625 * ((x_cand.T @ mxq(z, 0, "e4m3")))
    d_k2 = unpack_weight(d_words, d_scales)[np.arange(K)[:, None], runs(k2, K)]
    x_two = unpack_weight(x_words, x_scales)[:, unstriped(two)]
    b = 0.0625 * (d_k2.T @ x_two)
    return a + (sigmoid(b[:, unstriped(n3)] - b)) * (a[:, unstriped(n2)] - a)

@@ -1,0 +1,168 @@
+from contextlib import ExitStack
+
+import concourse.mybir as mybir
+
+K, T, S, G, H, C = 512, 1024, 256, 2048, 512, 512
+FLOPS = 2 * K * S * (H + C + H)
+
+F32 = mybir.dt.float32
+BF16 = mybir.dt.bfloat16
+I32 = mybir.dt.int32
+U32 = mybir.dt.uint32
+U16 = mybir.dt.uint16
+U8 = mybir.dt.uint8
+FP8X4 = mybir.dt.float8_e4m3fn_x4
+ALU = mybir.AluOpType
+ACT = mybir.ActivationFunctionType
+
+P = 128
+PACK = 4
+TILES = H // P
+
+
+def tile_picked_pqcjpullbsend_none_p_kernel(
+    tc, x_words, x_scales, d_words, d_scales, gs, offs, k1, n1, cand, two, k2, n2, n3, out
+):
+    nc = tc.nc
+    with ExitStack() as ctx:
+        sb = ctx.enter_context(tc.tile_pool(name="sb", bufs=1))
+        ps = ctx.enter_context(tc.psum_pool(name="ps", bufs=1))
+
+        def load_list(name, dram):
+            lst = sb.tile([P, dram.shape[1]], U16, name=name)
+            nc.sync.dma_start(lst[:], dram)
+            return lst
+
+        def gather(picked, table, lst):
+            nc.vector.tensor_copy(picked, table[:].indirect(lst[:]))
+
+        def gathered(name, table, lst, dtype, tag=None):
+            picked = sb.tile([P, 16 * lst.shape[1]], dtype, name=name, tag=tag or name, align_bytes=64)
+            gather(picked[:], table, lst)
+            return picked
+
+        def move_rows(queue, plane, source, rows):
+            for r in rows:
+                queue.dma_start(plane[r:P:32, :].bitcast(I32), source[8 * r : P : 32, :].bitcast(I32))
+
+        def product(acc, stat_words, stat_scales, t, mov_words, mov_scales):
+            cols = slice(t * P, (t + 1) * P)
+            nc.tensor.matmul_mx(
+                out=acc[:],
+                lhsT=stat_words[:, cols].bitcast(FP8X4),
+                lhsT_scale=stat_scales[:, cols],
+                rhs=mov_words[:].bitcast(FP8X4),
+                rhs_scale=mov_scales,
+                start=True,
+                stop=True,
+            )
+
+        dw = sb.tile([P, G], U32, name="dw")
+        xw = sb.tile([P, T], U32, name="xw")
+        dsc = sb.tile([P, G], U8, name="dsc")
+        xsc = sb.tile([P, T], U8, name="xsc")
+        nc.vector.memset(dsc[:].bitcast(I32), 0)
+        nc.gpsimd.memset(xsc[:].bitcast(I32), 0)
+        nc.scalar.dma_start(dsc[0:P:8, :].bitcast(I32), d_scales[0].bitcast(I32))
+        nc.scalar.dma_start(xsc[0:P:8, :].bitcast(I32), x_scales[0].bitcast(I32))
+        k1_l = load_list("k1_l", k1)
+        offs_l = load_list("offs_l", offs)
+        k2_l = load_list("k2_l", k2)
+        n1_l = load_list("n1_l", n1)
+        two_l = load_list("two_l", two)
+        nc.sync.dma_start(dw[:].bitcast(I32), d_words[0].rearrange("p n t -> p (n t)").bitcast(I32))
+        nc.sync.dma_start(xw[:].bitcast(I32), x_words[0].rearrange("p n t -> p (n t)").bitcast(I32))
+        cand_l = load_list("cand_l", cand)
+        n3_l = load_list("n3_l", n3)
+        n2_l = load_list("n2_l", n2)
+        g = sb.tile([P, PACK], F32, name="g")
+        nc.gpsimd.dma_start(g[:], gs.rearrange("(p t) o -> p (t o)", t=PACK))
+
+        g_pos = sb.tile([P, PACK], F32, name="g_pos")
+        g_neg = sb.tile([P, PACK], F32, name="g_neg")
+        nc.gpsimd.tensor_scalar(g_pos[:], g[:], 0.0625, 0.0, ALU.mult, ALU.add)
+        nc.gpsimd.tensor_scalar(g_neg[:], g[:], -0.03125, 0.0, ALU.mult, ALU.add)
+
+        k1_s = gathered("k1_s", dsc, k1_l, U8)
+        offs_s = gathered("offs_s", xsc, offs_l, U8)
+        h_s = sb.tile([P, H + S], U8, name="h_s", tag="bytes", align_bytes=64)
+        nc.vector.tensor_copy(
+            h_s[:, :H].rearrange("p (t m) -> p t m", t=PACK), k1_s[:].rearrange("p (m t) -> p t m", t=PACK)
+        )
+        nc.vector.tensor_copy(h_s[:, H:].bitcast(I32), offs_s[:].bitcast(I32))
+        move_rows(nc.scalar, h_s, h_s, (1, 2, 3))
+        k1_w = gathered("k1_w", dw, k1_l, U32, "undealt")
+        k1_wd = sb.tile([P, H], U32, name="k1_wd", tag="stationary", align_bytes=64)
+        nc.vector.tensor_copy(
+            k1_wd[:].rearrange("p (t m) -> p m t", t=PACK), k1_w[:].rearrange("p (m t) -> p m t", t=PACK)
+        )
+        offs_w = gathered("offs_w", xw, offs_l, U32, "moving")
+        h_ps = [ps.tile([P, S], F32, name=f"h{t}", tag=f"ha{t}") for t in range(TILES)]
+        for t in range(TILES):
+            product(h_ps[t], k1_wd, h_s[:, :H], t, offs_w, h_s[:, H:])
+
+        two_w = gathered("two_w", xw, two_l, U32, "undealt")
+        b_g = sb.tile([P, H + S], U8, name="b_g", tag="moving", align_bytes=64)
+        b_s = sb.tile([P, H + S], U8, name="b_s", align_bytes=64)
+        cand_s = sb.tile([P, C], U8, name="cand_s", align_bytes=64)
+        nc.gpsimd.memset(b_s[:].bitcast(I32), 0)
+        nc.gpsimd.memset(cand_s[:].bitcast(I32), 0)
+
+        b_rl = [sb.tile([P, 2 * S], F32, name=f"b_rl{t}") for t in range(TILES)]
+        ds = [sb.tile([P, 2 * S], F32, name=f"ds{t}") for t in range(TILES)]
+
+        def send(t):
+            nc.vector.tensor_scalar(b_rl[t][:, S:], h_ps[t][:], 0.0, g_pos[:, t : t + 1], ALU.max, ALU.mult)
+            nc.scalar.activation(ds[t][:].indirect(n1_l[:]), b_rl[t][:, S:], ACT.Copy)
+
+        send(0)
+        gather(b_g[:, :H], dsc, k2_l)
+        send(1)
+        gather(b_g[:, H:], xsc, two_l)
+        move_rows(nc.sync, b_s, b_g, range(4))
+        send(2)
+        k2_w = gathered("k2_w", dw, k2_l, U32, "stationary")
+        send(3)
+        b_ps = [ps.tile([P, S], F32, name=f"b{t}", tag=f"b{t}") for t in range(TILES)]
+        for t in range(TILES):
+            product(b_ps[t], k2_w, b_s[:, :H], t, two_w, b_s[:, H:])
+        cand_g = gathered("cand_g", xsc, cand_l, U8, "bytes")
+        move_rows(nc.sync, cand_s, cand_g, range(4))
+        cand_w = gathered("cand_w", xw, cand_l, U32, "moving")
+        for t in range(TILES):
+            nc.vector.tensor_copy(b_rl[t][:, :S], b_ps[t][:])
+
+        z = sb.tile([P, PACK, S], BF16, name="z", tag="stationary", align_bytes=64)
+        for t in range(TILES):
+            nc.vector.scalar_tensor_tensor(
+                z[:, t, :], h_ps[t][:], g_neg[:, t : t + 1], ds[t][:, :S], ALU.mult, ALU.add
+            )
+        z_il = sb.tile([P, S * PACK], BF16, name="z_il", align_bytes=64)
+        nc.vector.tensor_copy(z_il[:].rearrange("p (j t) -> p j t", t=PACK), z[:].rearrange("p t j -> p j t"))
+        z_w = sb.tile([P, S], U32, name="z_w", align_bytes=64)
+        z_s = sb.tile([P, S], U8, name="z_s", align_bytes=64)
+        nc.vector.quantize_mx(out=z_w[:].bitcast(FP8X4), scales=z_s[:], in_=z_il[:])
+        a_ps = [ps.tile([P, S], F32, name=f"a{t}", tag=f"ha{t}") for t in range(TILES)]
+        for t in range(TILES):
+            product(a_ps[t], cand_w, cand_s, t, z_w, z_s[:])
+
+        a_df = [sb.tile([P, 2 * S], F32, name=f"a_df{t}") for t in range(TILES)]
+        b_got = [sb.tile([P, S], F32, name=f"b_got{t}") for t in range(TILES)]
+        th = [sb.tile([P, S], F32, name=f"th{t}") for t in range(TILES)]
+        for t in range(TILES):
+            nc.scalar.activation(b_got[t][:], b_rl[t][:].indirect(n3_l[:]), ACT.Copy)
+        for t in range(TILES):
+            nc.vector.tensor_tensor(a_df[t][:, S:], b_got[t][:], b_rl[t][:, :S], ALU.subtract)
+            nc.scalar.activation(th[t][:], a_df[t][:, S:], ACT.Tanh, scale=0.03125)
+
+        for t in range(TILES):
+            nc.scalar.activation(a_df[t][:, :S], a_ps[t][:], ACT.Copy, scale=0.03125)
+            a_got = sb.tile([P, S], F32, name=f"a_got{t}")
+            nc.scalar.activation(a_got[:], a_df[t][:].indirect(n2_l[:]), ACT.Copy)
+            stay = sb.tile([P, S], F32, name=f"stay{t}")
+            nc.vector.scalar_tensor_tensor(stay[:], th[t][:], 1.0, a_ps[t][:], ALU.subtract, ALU.mult)
+            come = sb.tile([P, S], F32, name=f"come{t}")
+            nc.vector.scalar_tensor_tensor(come[:], th[t][:], 1.0, a_got[:], ALU.add, ALU.mult)
+            res = sb.tile([P, S], F32, name=f"res{t}")
+            nc.vector.scalar_tensor_tensor(res[:], stay[:], -0.03125, come[:], ALU.mult, ALU.add)
+            nc.sync.dma_start(out[t * P : (t + 1) * P, :], res[:])

@@ -51,7 +51,7 @@ def tile_picked_pqcjpullbsend_none_p_kernel(
                 out=acc[:],
                 lhsT=stat_words[:, cols].bitcast(FP8X4),
                 lhsT_scale=stat_scales[:, cols],
-                rhs=mov_words[:].bitcast(FP8X4),
+                rhs=mov_words.bitcast(FP8X4),
                 rhs_scale=mov_scales,
                 start=True,
                 stop=True,
@@ -63,13 +63,13 @@ def tile_picked_pqcjpullbsend_none_p_kernel(
         xsc = sb.tile([P, T], U8, name="xsc")
         nc.vector.memset(dsc[:].bitcast(I32), 0)
         nc.gpsimd.memset(xsc[:].bitcast(I32), 0)
-        nc.scalar.dma_start(dsc[0:P:8, :].bitcast(I32), d_scales[0].bitcast(I32))
-        nc.scalar.dma_start(xsc[0:P:8, :].bitcast(I32), x_scales[0].bitcast(I32))
         k1_l = load_list("k1_l", k1)
+        nc.scalar.dma_start(dsc[0:P:8, :].bitcast(I32), d_scales[0].bitcast(I32))
         offs_l = load_list("offs_l", offs)
+        nc.sync.dma_start(xsc[0:P:8, :].bitcast(I32), x_scales[0].bitcast(I32))
+        two_l = load_list("two_l", two)
         k2_l = load_list("k2_l", k2)
         n1_l = load_list("n1_l", n1)
-        two_l = load_list("two_l", two)
         nc.sync.dma_start(dw[:].bitcast(I32), d_words[0].rearrange("p n t -> p (n t)").bitcast(I32))
         nc.sync.dma_start(xw[:].bitcast(I32), x_words[0].rearrange("p n t -> p (n t)").bitcast(I32))
         cand_l = load_list("cand_l", cand)
@@ -83,30 +83,32 @@ def tile_picked_pqcjpullbsend_none_p_kernel(
         nc.gpsimd.tensor_scalar(g_pos[:], g[:], 0.0625, 0.0, ALU.mult, ALU.add)
         nc.gpsimd.tensor_scalar(g_neg[:], g[:], -0.03125, 0.0, ALU.mult, ALU.add)
 
-        k1_s = gathered("k1_s", dsc, k1_l, U8)
-        offs_s = gathered("offs_s", xsc, offs_l, U8)
-        h_s = sb.tile([P, H + S], U8, name="h_s", tag="bytes", align_bytes=64)
-        nc.vector.tensor_copy(
-            h_s[:, :H].rearrange("p (t m) -> p t m", t=PACK), k1_s[:].rearrange("p (m t) -> p t m", t=PACK)
-        )
-        nc.vector.tensor_copy(h_s[:, H:].bitcast(I32), offs_s[:].bitcast(I32))
-        move_rows(nc.scalar, h_s, h_s, (1, 2, 3))
-        k1_w = gathered("k1_w", dw, k1_l, U32, "undealt")
+        early_g = sb.tile([P, H + 2 * S], U8, name="early_g", tag="picked", align_bytes=64)
+        early_s = sb.tile([P, H + 2 * S], U8, name="early_s", align_bytes=64)
+        k2_s = sb.tile([P, H], U8, name="k2_s", align_bytes=64)
+        cand_s = sb.tile([P, C], U8, name="cand_s", align_bytes=64)
+        for plane in (early_s, k2_s, cand_s):
+            nc.gpsimd.memset(plane[:].bitcast(I32), 0)
+        gather(early_g[:, :H], dsc, k1_l)
+        gather(early_g[:, H : H + S], xsc, offs_l)
+        gather(early_g[:, H + S :], xsc, two_l)
+        move_rows(nc.scalar, early_s, early_g, (0, 1))
+        move_rows(nc.sync, early_s, early_g, (2, 3))
+        k1_w = gathered("k1_w", dw, k1_l, U32, "words")
         k1_wd = sb.tile([P, H], U32, name="k1_wd", tag="stationary", align_bytes=64)
         nc.vector.tensor_copy(
             k1_wd[:].rearrange("p (t m) -> p m t", t=PACK), k1_w[:].rearrange("p (m t) -> p m t", t=PACK)
         )
-        offs_w = gathered("offs_w", xw, offs_l, U32, "moving")
+        offs_w = gathered("offs_w", xw, offs_l, U32, "words")
+        k1_s = sb.tile([P, H], U8, name="k1_s", tag="bytes", align_bytes=64)
+        nc.vector.tensor_copy(
+            k1_s[:].rearrange("p (t m) -> p t m", t=PACK), early_s[:, :H].rearrange("p (m t) -> p t m", t=PACK)
+        )
         h_ps = [ps.tile([P, S], F32, name=f"h{t}", tag=f"ha{t}") for t in range(TILES)]
         for t in range(TILES):
-            product(h_ps[t], k1_wd, h_s[:, :H], t, offs_w, h_s[:, H:])
-
-        two_w = gathered("two_w", xw, two_l, U32, "undealt")
-        b_g = sb.tile([P, H + S], U8, name="b_g", tag="moving", align_bytes=64)
-        b_s = sb.tile([P, H + S], U8, name="b_s", align_bytes=64)
-        cand_s = sb.tile([P, C], U8, name="cand_s", align_bytes=64)
-        nc.gpsimd.memset(b_s[:].bitcast(I32), 0)
-        nc.gpsimd.memset(cand_s[:].bitcast(I32), 0)
+            product(h_ps[t], k1_wd, k1_s, t, offs_w[:], early_s[:, H : H + S])
+        k2_g = gathered("k2_g", dsc, k2_l, U8, "picked")
+        move_rows(nc.sync, k2_s, k2_g, range(4))
 
         b_rl = [sb.tile([P, 2 * S], F32, name=f"b_rl{t}") for t in range(TILES)]
         ds = [sb.tile([P, 2 * S], F32, name=f"ds{t}") for t in range(TILES)]
@@ -116,19 +118,17 @@ def tile_picked_pqcjpullbsend_none_p_kernel(
             nc.scalar.activation(ds[t][:].indirect(n1_l[:]), b_rl[t][:, S:], ACT.Copy)
 
         send(0)
-        gather(b_g[:, :H], dsc, k2_l)
-        send(1)
-        gather(b_g[:, H:], xsc, two_l)
-        move_rows(nc.sync, b_s, b_g, range(4))
-        send(2)
         k2_w = gathered("k2_w", dw, k2_l, U32, "stationary")
-        send(3)
-        b_ps = [ps.tile([P, S], F32, name=f"b{t}", tag=f"b{t}") for t in range(TILES)]
-        for t in range(TILES):
-            product(b_ps[t], k2_w, b_s[:, :H], t, two_w, b_s[:, H:])
+        send(1)
         cand_g = gathered("cand_g", xsc, cand_l, U8, "bytes")
         move_rows(nc.sync, cand_s, cand_g, range(4))
-        cand_w = gathered("cand_w", xw, cand_l, U32, "moving")
+        send(2)
+        two_w = gathered("two_w", xw, two_l, U32, "words")
+        b_ps = [ps.tile([P, S], F32, name=f"b{t}", tag=f"b{t}") for t in range(TILES)]
+        for t in range(TILES):
+            product(b_ps[t], k2_w, k2_s, t, two_w[:], early_s[:, H + S :])
+        send(3)
+        cand_w = gathered("cand_w", xw, cand_l, U32, "picked")
         for t in range(TILES):
             nc.vector.tensor_copy(b_rl[t][:, :S], b_ps[t][:])
 
@@ -137,32 +137,36 @@ def tile_picked_pqcjpullbsend_none_p_kernel(
             nc.vector.scalar_tensor_tensor(
                 z[:, t, :], h_ps[t][:], g_neg[:, t : t + 1], ds[t][:, :S], ALU.mult, ALU.add
             )
-        z_il = sb.tile([P, S * PACK], BF16, name="z_il", align_bytes=64)
+        z_il = sb.tile([P, S * PACK], BF16, name="z_il", tag="z_diff", align_bytes=64)
         nc.vector.tensor_copy(z_il[:].rearrange("p (j t) -> p j t", t=PACK), z[:].rearrange("p t j -> p j t"))
         z_w = sb.tile([P, S], U32, name="z_w", align_bytes=64)
         z_s = sb.tile([P, S], U8, name="z_s", align_bytes=64)
         nc.vector.quantize_mx(out=z_w[:].bitcast(FP8X4), scales=z_s[:], in_=z_il[:])
         a_ps = [ps.tile([P, S], F32, name=f"a{t}", tag=f"ha{t}") for t in range(TILES)]
         for t in range(TILES):
-            product(a_ps[t], cand_w, cand_s, t, z_w, z_s[:])
+            product(a_ps[t], cand_w, cand_s, t, z_w[:], z_s[:])
 
-        a_df = [sb.tile([P, 2 * S], F32, name=f"a_df{t}") for t in range(TILES)]
+        a_th = [sb.tile([P, 2 * S], F32, name=f"a_th{t}") for t in range(TILES)]
         b_got = [sb.tile([P, S], F32, name=f"b_got{t}") for t in range(TILES)]
-        th = [sb.tile([P, S], F32, name=f"th{t}") for t in range(TILES)]
+        diff = sb.tile([P, TILES * S], F32, name="diff", tag="z_diff", align_bytes=64)
         for t in range(TILES):
             nc.scalar.activation(b_got[t][:], b_rl[t][:].indirect(n3_l[:]), ACT.Copy)
         for t in range(TILES):
-            nc.vector.tensor_tensor(a_df[t][:, S:], b_got[t][:], b_rl[t][:, :S], ALU.subtract)
-            nc.scalar.activation(th[t][:], a_df[t][:, S:], ACT.Tanh, scale=0.03125)
+            cols = slice(t * S, (t + 1) * S)
+            nc.vector.tensor_tensor(diff[:, cols], b_got[t][:], b_rl[t][:, :S], ALU.subtract)
+            nc.scalar.activation(a_th[t][:, S:], diff[:, cols], ACT.Tanh, scale=0.03125)
 
         for t in range(TILES):
-            nc.scalar.activation(a_df[t][:, :S], a_ps[t][:], ACT.Copy, scale=0.03125)
+            if t < 2:
+                nc.vector.tensor_scalar(a_th[t][:, :S], a_ps[t][:], 0.03125, None, ALU.mult)
+            else:
+                nc.scalar.activation(a_th[t][:, :S], a_ps[t][:], ACT.Copy, scale=0.03125)
             a_got = sb.tile([P, S], F32, name=f"a_got{t}")
-            nc.scalar.activation(a_got[:], a_df[t][:].indirect(n2_l[:]), ACT.Copy)
+            nc.scalar.activation(a_got[:], a_th[t][:].indirect(n2_l[:]), ACT.Copy)
             stay = sb.tile([P, S], F32, name=f"stay{t}")
-            nc.vector.scalar_tensor_tensor(stay[:], th[t][:], 1.0, a_ps[t][:], ALU.subtract, ALU.mult)
+            nc.vector.scalar_tensor_tensor(stay[:], a_th[t][:, S:], 1.0, a_ps[t][:], ALU.subtract, ALU.mult)
             come = sb.tile([P, S], F32, name=f"come{t}")
-            nc.vector.scalar_tensor_tensor(come[:], th[t][:], 1.0, a_got[:], ALU.add, ALU.mult)
+            nc.vector.scalar_tensor_tensor(come[:], a_th[t][:, S:], 1.0, a_got[:], ALU.add, ALU.mult)
             res = sb.tile([P, S], F32, name=f"res{t}")
             nc.vector.scalar_tensor_tensor(res[:], stay[:], -0.03125, come[:], ALU.mult, ALU.add)
             nc.sync.dma_start(out[t * P : (t + 1) * P, :], res[:])

@@ -48,7 +48,7 @@ def tile_picked_pqcjpullbsend_none_p_kernel(
         def product(acc, stat_words, stat_scales, t, mov_words, mov_scales):
             cols = slice(t * P, (t + 1) * P)
             nc.tensor.matmul_mx(
-                out=acc[:],
+                out=acc,
                 lhsT=stat_words[:, cols].bitcast(FP8X4),
                 lhsT_scale=stat_scales[:, cols],
                 rhs=mov_words.bitcast(FP8X4),
@@ -83,17 +83,19 @@ def tile_picked_pqcjpullbsend_none_p_kernel(
         nc.gpsimd.tensor_scalar(g_pos[:], g[:], 0.0625, 0.0, ALU.mult, ALU.add)
         nc.gpsimd.tensor_scalar(g_neg[:], g[:], -0.03125, 0.0, ALU.mult, ALU.add)
 
-        early_g = sb.tile([P, H + 2 * S], U8, name="early_g", tag="picked", align_bytes=64)
-        early_s = sb.tile([P, H + 2 * S], U8, name="early_s", align_bytes=64)
+        early_g = sb.tile([P, H + S], U8, name="early_g", tag="picked", align_bytes=64)
+        early_s = sb.tile([P, H + S], U8, name="early_s", align_bytes=64)
+        two_s = sb.tile([P, S], U8, name="two_s", align_bytes=64)
         k2_s = sb.tile([P, H], U8, name="k2_s", align_bytes=64)
         cand_s = sb.tile([P, C], U8, name="cand_s", align_bytes=64)
-        for plane in (early_s, k2_s, cand_s):
+        for plane in (early_s, two_s, k2_s, cand_s):
             nc.gpsimd.memset(plane[:].bitcast(I32), 0)
         gather(early_g[:, :H], dsc, k1_l)
-        gather(early_g[:, H : H + S], xsc, offs_l)
-        gather(early_g[:, H + S :], xsc, two_l)
+        gather(early_g[:, H:], xsc, offs_l)
         move_rows(nc.scalar, early_s, early_g, (0, 1))
         move_rows(nc.sync, early_s, early_g, (2, 3))
+        two_g = gathered("two_g", xsc, two_l, U8)
+        move_rows(nc.sync, two_s, two_g, range(4))
         k1_w = gathered("k1_w", dw, k1_l, U32, "words")
         k1_wd = sb.tile([P, H], U32, name="k1_wd", tag="stationary", align_bytes=64)
         nc.vector.tensor_copy(
@@ -101,36 +103,35 @@ def tile_picked_pqcjpullbsend_none_p_kernel(
         )
         offs_w = gathered("offs_w", xw, offs_l, U32, "words")
         k1_s = sb.tile([P, H], U8, name="k1_s", tag="bytes", align_bytes=64)
-        nc.vector.tensor_copy(
-            k1_s[:].rearrange("p (t m) -> p t m", t=PACK), early_s[:, :H].rearrange("p (m t) -> p t m", t=PACK)
-        )
-        h_ps = [ps.tile([P, S], F32, name=f"h{t}", tag=f"ha{t}") for t in range(TILES)]
+        k1_by_tile = early_s[:, :H].rearrange("p (m t) -> p t m", t=PACK)
+        nc.vector.tensor_copy(k1_s[:, :P], k1_by_tile[:, 0, :])
+        nc.vector.tensor_copy(k1_s[:, P:].rearrange("p (t m) -> p t m", m=P), k1_by_tile[:, 1:, :])
+        h_ps = [ps.tile([P, S], F32, name=f"h{t}") for t in range(TILES)]
         for t in range(TILES):
-            product(h_ps[t], k1_wd, k1_s, t, offs_w[:], early_s[:, H : H + S])
-        k2_g = gathered("k2_g", dsc, k2_l, U8, "picked")
-        move_rows(nc.sync, k2_s, k2_g, range(4))
+            product(h_ps[t][:], k1_wd, k1_s, t, offs_w[:], early_s[:, H:])
+        two_w = gathered("two_w", xw, two_l, U32, "picked")
 
-        b_rl = [sb.tile([P, 2 * S], F32, name=f"b_rl{t}") for t in range(TILES)]
+        b_rl = sb.tile([P, 2 * TILES * S], F32, name="b_rl")
+        rl = [b_rl[:, (TILES + t) * S : (TILES + t + 1) * S] for t in range(TILES)]
         ds = [sb.tile([P, 2 * S], F32, name=f"ds{t}") for t in range(TILES)]
 
         def send(t):
-            nc.vector.tensor_scalar(b_rl[t][:, S:], h_ps[t][:], 0.0, g_pos[:, t : t + 1], ALU.max, ALU.mult)
-            nc.scalar.activation(ds[t][:].indirect(n1_l[:]), b_rl[t][:, S:], ACT.Copy)
+            nc.vector.tensor_scalar(rl[t], h_ps[t][:], 0.0, g_pos[:, t : t + 1], ALU.max, ALU.mult)
+            nc.scalar.activation(ds[t][:].indirect(n1_l[:]), rl[t], ACT.Copy)
 
         send(0)
-        k2_w = gathered("k2_w", dw, k2_l, U32, "stationary")
+        k2_g = gathered("k2_g", dsc, k2_l, U8, "words")
+        move_rows(nc.sync, k2_s, k2_g, range(4))
         send(1)
+        k2_w = gathered("k2_w", dw, k2_l, U32, "stationary")
+        b_ps = [ps.tile([P, 2 * S], F32, name=f"b{u}") for u in range(2)]
+        for t in range(TILES):
+            product(b_ps[t // 2][:, (t % 2) * S : (t % 2 + 1) * S], k2_w, k2_s, t, two_w[:], two_s[:])
+        send(2)
         cand_g = gathered("cand_g", xsc, cand_l, U8, "bytes")
         move_rows(nc.sync, cand_s, cand_g, range(4))
-        send(2)
-        two_w = gathered("two_w", xw, two_l, U32, "words")
-        b_ps = [ps.tile([P, S], F32, name=f"b{t}", tag=f"b{t}") for t in range(TILES)]
-        for t in range(TILES):
-            product(b_ps[t], k2_w, k2_s, t, two_w[:], early_s[:, H + S :])
         send(3)
-        cand_w = gathered("cand_w", xw, cand_l, U32, "picked")
-        for t in range(TILES):
-            nc.vector.tensor_copy(b_rl[t][:, :S], b_ps[t][:])
+        cand_w = gathered("cand_w", xw, cand_l, U32, "words")
 
         z = sb.tile([P, PACK, S], BF16, name="z", tag="stationary", align_bytes=64)
         for t in range(TILES):
@@ -142,31 +143,55 @@ def tile_picked_pqcjpullbsend_none_p_kernel(
         z_w = sb.tile([P, S], U32, name="z_w", align_bytes=64)
         z_s = sb.tile([P, S], U8, name="z_s", align_bytes=64)
         nc.vector.quantize_mx(out=z_w[:].bitcast(FP8X4), scales=z_s[:], in_=z_il[:])
-        a_ps = [ps.tile([P, S], F32, name=f"a{t}", tag=f"ha{t}") for t in range(TILES)]
+        a_ps = [ps.tile([P, 2 * S], F32, name=f"a{u}") for u in range(2)]
         for t in range(TILES):
-            product(a_ps[t], cand_w, cand_s, t, z_w[:], z_s[:])
+            product(a_ps[t // 2][:, (t % 2) * S : (t % 2 + 1) * S], cand_w, cand_s, t, z_w[:], z_s[:])
 
-        a_th = [sb.tile([P, 2 * S], F32, name=f"a_th{t}") for t in range(TILES)]
-        b_got = [sb.tile([P, S], F32, name=f"b_got{t}") for t in range(TILES)]
+        def cols(first, count):
+            return slice(first * S, (first + count) * S)
+
+        a_th = sb.tile([P, 2 * TILES * S], F32, name="a_th")
+        b_got = sb.tile([P, TILES * S], F32, name="b_got")
+        a_got = sb.tile([P, TILES * S], F32, name="a_got")
         diff = sb.tile([P, TILES * S], F32, name="diff", tag="z_diff", align_bytes=64)
-        for t in range(TILES):
-            nc.scalar.activation(b_got[t][:], b_rl[t][:].indirect(n3_l[:]), ACT.Copy)
-        for t in range(TILES):
-            cols = slice(t * S, (t + 1) * S)
-            nc.vector.tensor_tensor(diff[:, cols], b_got[t][:], b_rl[t][:, :S], ALU.subtract)
-            nc.scalar.activation(a_th[t][:, S:], diff[:, cols], ACT.Tanh, scale=0.03125)
+        stay = sb.tile([P, TILES * S], F32, name="stay")
+        come = sb.tile([P, TILES * S], F32, name="come")
+        res = sb.tile([P, TILES * S], F32, name="res")
+        out_rows = out.rearrange("(t p) j -> p t j", p=P)
 
+        for u in range(2):
+            nc.scalar.activation(b_rl[:, cols(2 * u, 2)], b_ps[u][:], ACT.Copy)
         for t in range(TILES):
-            if t < 2:
-                nc.vector.tensor_scalar(a_th[t][:, :S], a_ps[t][:], 0.03125, None, ALU.mult)
-            else:
-                nc.scalar.activation(a_th[t][:, :S], a_ps[t][:], ACT.Copy, scale=0.03125)
-            a_got = sb.tile([P, S], F32, name=f"a_got{t}")
-            nc.scalar.activation(a_got[:], a_th[t][:].indirect(n2_l[:]), ACT.Copy)
-            stay = sb.tile([P, S], F32, name=f"stay{t}")
-            nc.vector.scalar_tensor_tensor(stay[:], a_th[t][:, S:], 1.0, a_ps[t][:], ALU.subtract, ALU.mult)
-            come = sb.tile([P, S], F32, name=f"come{t}")
-            nc.vector.scalar_tensor_tensor(come[:], a_th[t][:, S:], 1.0, a_got[:], ALU.add, ALU.mult)
-            res = sb.tile([P, S], F32, name=f"res{t}")
-            nc.vector.scalar_tensor_tensor(res[:], stay[:], -0.03125, come[:], ALU.mult, ALU.add)
-            nc.sync.dma_start(out[t * P : (t + 1) * P, :], res[:])
+            nc.scalar.activation(b_got[:, cols(t, 1)], b_rl[:, cols(t, 2)].indirect(n3_l[:]), ACT.Copy)
+        for u in range(2):
+            pair = cols(2 * u, 2)
+            nc.vector.tensor_tensor(diff[:, pair], b_got[:, pair], b_rl[:, pair], ALU.subtract)
+            nc.scalar.activation(a_th[:, cols(TILES + 2 * u, 2)], diff[:, pair], ACT.Tanh, scale=0.03125)
+            nc.vector.tensor_scalar(a_th[:, pair], a_ps[u][:], 0.03125, None, ALU.mult)
+        for t in range(TILES):
+            nc.scalar.activation(a_got[:, cols(t, 1)], a_th[:, cols(t, 2)].indirect(n2_l[:]), ACT.Copy)
+
+        def keep_part(u):
+            nc.vector.scalar_tensor_tensor(
+                stay[:, cols(2 * u, 2)], a_th[:, cols(TILES + 2 * u, 2)], 1.0, a_ps[u][:], ALU.subtract, ALU.mult
+            )
+
+        def fetched_part(first, count):
+            span = cols(first, count)
+            nc.vector.scalar_tensor_tensor(
+                come[:, span], a_th[:, cols(TILES + first, count)], 1.0, a_got[:, span], ALU.add, ALU.mult
+            )
+
+        def finish(first, count):
+            span = cols(first, count)
+            nc.vector.scalar_tensor_tensor(res[:, span], stay[:, span], -0.03125, come[:, span], ALU.mult, ALU.add)
+            nc.sync.dma_start(out_rows[:, first : first + count, :], res[:, span].rearrange("p (t j) -> p t j", j=S))
+
+        keep_part(0)
+        fetched_part(0, 2)
+        keep_part(1)
+        finish(0, 2)
+        fetched_part(2, 1)
+        fetched_part(3, 1)
+        finish(2, 1)
+        finish(3, 1)

@@ -133,16 +133,27 @@ def tile_picked_pqcjpullbsend_none_p_kernel(
         send(3)
         cand_w = gathered("cand_w", xw, cand_l, U32, "words")
 
-        z = sb.tile([P, PACK, S], BF16, name="z", tag="stationary", align_bytes=64)
+        z = sb.tile([P, 2, PACK, S // 2], BF16, name="z", tag="stationary", align_bytes=64)
         for t in range(TILES):
-            nc.vector.scalar_tensor_tensor(
-                z[:, t, :], h_ps[t][:], g_neg[:, t : t + 1], ds[t][:, :S], ALU.mult, ALU.add
-            )
+            h_halves = h_ps[t][:].rearrange("p (u j) -> p u j", u=2)
+            ds_halves = ds[t][:, :S].rearrange("p (u j) -> p u j", u=2)
+            for us in [slice(0, 2)] if t < TILES - 1 else [slice(0, 1), slice(1, 2)]:
+                nc.vector.scalar_tensor_tensor(
+                    z[:, us, t, :], h_halves[:, us, :], g_neg[:, t : t + 1], ds_halves[:, us, :], ALU.mult, ALU.add
+                )
         z_il = sb.tile([P, S * PACK], BF16, name="z_il", tag="z_diff", align_bytes=64)
-        nc.vector.tensor_copy(z_il[:].rearrange("p (j t) -> p j t", t=PACK), z[:].rearrange("p t j -> p j t"))
         z_w = sb.tile([P, S], U32, name="z_w", align_bytes=64)
         z_s = sb.tile([P, S], U8, name="z_s", align_bytes=64)
-        nc.vector.quantize_mx(out=z_w[:].bitcast(FP8X4), scales=z_s[:], in_=z_il[:])
+        for u in range(2):
+            nc.vector.tensor_copy(
+                z_il[:, u * 2 * S : (u + 1) * 2 * S].rearrange("p (c i t) -> p c t i", i=4, t=PACK),
+                z[:, u, :, :].rearrange("p t (c i) -> p c t i", i=4),
+            )
+        for u in range(2):
+            half = slice(u * S // 2, (u + 1) * S // 2)
+            nc.vector.quantize_mx(
+                out=z_w[:, half].bitcast(FP8X4), scales=z_s[:, half], in_=z_il[:, u * 2 * S : (u + 1) * 2 * S]
+            )
         a_ps = [ps.tile([P, 2 * S], F32, name=f"a{u}") for u in range(2)]
         for t in range(TILES):
             product(a_ps[t // 2][:, (t % 2) * S : (t % 2 + 1) * S], cand_w, cand_s, t, z_w[:], z_s[:])

from contextlib import ExitStack

import concourse.mybir as mybir

K, T, S, G, H, C = 512, 1024, 256, 2048, 512, 512
FLOPS = 2 * K * S * (H + C + H)

F32 = mybir.dt.float32
BF16 = mybir.dt.bfloat16
I32 = mybir.dt.int32
U32 = mybir.dt.uint32
U16 = mybir.dt.uint16
U8 = mybir.dt.uint8
FP8X4 = mybir.dt.float8_e4m3fn_x4
ALU = mybir.AluOpType
ACT = mybir.ActivationFunctionType

P = 128
PACK = 4
TILES = H // P


def tile_picked_pqcjpullbsend_none_p_kernel(
    tc, x_words, x_scales, d_words, d_scales, gs, offs, k1, n1, cand, two, k2, n2, n3, out
):
    nc = tc.nc
    with ExitStack() as ctx:
        sb = ctx.enter_context(tc.tile_pool(name="sb", bufs=1))
        ps = ctx.enter_context(tc.psum_pool(name="ps", bufs=1))

        def load_list(name, dram):
            lst = sb.tile([P, dram.shape[1]], U16, name=name)
            nc.sync.dma_start(lst[:], dram)
            return lst

        def gather(picked, table, lst):
            nc.vector.tensor_copy(picked, table[:].indirect(lst[:]))

        def gathered(name, table, lst, dtype, tag=None):
            picked = sb.tile([P, 16 * lst.shape[1]], dtype, name=name, tag=tag or name, align_bytes=64)
            gather(picked[:], table, lst)
            return picked

        def move_rows(queue, plane, source, rows):
            for r in rows:
                queue.dma_start(plane[r:P:32, :].bitcast(I32), source[8 * r : P : 32, :].bitcast(I32))

        def product(acc, stat_words, stat_scales, t, mov_words, mov_scales):
            cols = slice(t * P, (t + 1) * P)
            nc.tensor.matmul_mx(
                out=acc,
                lhsT=stat_words[:, cols].bitcast(FP8X4),
                lhsT_scale=stat_scales[:, cols],
                rhs=mov_words.bitcast(FP8X4),
                rhs_scale=mov_scales,
                start=True,
                stop=True,
            )

        dw = sb.tile([P, G], U32, name="dw")
        xw = sb.tile([P, T], U32, name="xw")
        dsc = sb.tile([P, G], U8, name="dsc")
        xsc = sb.tile([P, T], U8, name="xsc")
        nc.vector.memset(dsc[:].bitcast(I32), 0)
        nc.gpsimd.memset(xsc[:].bitcast(I32), 0)
        k1_l = load_list("k1_l", k1)
        nc.scalar.dma_start(dsc[0:P:8, :].bitcast(I32), d_scales[0].bitcast(I32))
        offs_l = load_list("offs_l", offs)
        nc.sync.dma_start(xsc[0:P:8, :].bitcast(I32), x_scales[0].bitcast(I32))
        two_l = load_list("two_l", two)
        k2_l = load_list("k2_l", k2)
        n1_l = load_list("n1_l", n1)
        nc.sync.dma_start(dw[:].bitcast(I32), d_words[0].rearrange("p n t -> p (n t)").bitcast(I32))
        nc.sync.dma_start(xw[:].bitcast(I32), x_words[0].rearrange("p n t -> p (n t)").bitcast(I32))
        cand_l = load_list("cand_l", cand)
        n3_l = load_list("n3_l", n3)
        n2_l = load_list("n2_l", n2)
        g = sb.tile([P, PACK], F32, name="g")
        nc.gpsimd.dma_start(g[:], gs.rearrange("(p t) o -> p (t o)", t=PACK))

        g_pos = sb.tile([P, PACK], F32, name="g_pos")
        g_neg = sb.tile([P, PACK], F32, name="g_neg")
        nc.gpsimd.tensor_scalar(g_pos[:], g[:], 0.0625, 0.0, ALU.mult, ALU.add)
        nc.gpsimd.tensor_scalar(g_neg[:], g[:], -0.03125, 0.0, ALU.mult, ALU.add)

        early_g = sb.tile([P, H + S], U8, name="early_g", tag="picked", align_bytes=64)
        early_s = sb.tile([P, H + S], U8, name="early_s", align_bytes=64)
        two_s = sb.tile([P, S], U8, name="two_s", align_bytes=64)
        k2_s = sb.tile([P, H], U8, name="k2_s", align_bytes=64)
        cand_s = sb.tile([P, C], U8, name="cand_s", align_bytes=64)
        for plane in (early_s, two_s, k2_s, cand_s):
            nc.gpsimd.memset(plane[:].bitcast(I32), 0)
        gather(early_g[:, :H], dsc, k1_l)
        gather(early_g[:, H:], xsc, offs_l)
        move_rows(nc.scalar, early_s, early_g, (0, 1))
        move_rows(nc.sync, early_s, early_g, (2, 3))
        two_g = gathered("two_g", xsc, two_l, U8)
        move_rows(nc.sync, two_s, two_g, range(4))
        k1_w = gathered("k1_w", dw, k1_l, U32, "words")
        k1_wd = sb.tile([P, H], U32, name="k1_wd", tag="stationary", align_bytes=64)
        nc.vector.tensor_copy(
            k1_wd[:].rearrange("p (t m) -> p m t", t=PACK), k1_w[:].rearrange("p (m t) -> p m t", t=PACK)
        )
        offs_w = gathered("offs_w", xw, offs_l, U32, "words")
        k1_s = sb.tile([P, H], U8, name="k1_s", tag="bytes", align_bytes=64)
        k1_by_tile = early_s[:, :H].rearrange("p (m t) -> p t m", t=PACK)
        nc.vector.tensor_copy(k1_s[:, :P], k1_by_tile[:, 0, :])
        nc.vector.tensor_copy(k1_s[:, P:].rearrange("p (t m) -> p t m", m=P), k1_by_tile[:, 1:, :])
        h_ps = [ps.tile([P, S], F32, name=f"h{t}") for t in range(TILES)]
        for t in range(TILES):
            product(h_ps[t][:], k1_wd, k1_s, t, offs_w[:], early_s[:, H:])
        two_w = gathered("two_w", xw, two_l, U32, "picked")

        b_rl = sb.tile([P, 2 * TILES * S], F32, name="b_rl")
        rl = [b_rl[:, (TILES + t) * S : (TILES + t + 1) * S] for t in range(TILES)]
        ds = [sb.tile([P, 2 * S], F32, name=f"ds{t}") for t in range(TILES)]

        def send(t):
            nc.vector.tensor_scalar(rl[t], h_ps[t][:], 0.0, g_pos[:, t : t + 1], ALU.max, ALU.mult)
            nc.scalar.activation(ds[t][:].indirect(n1_l[:]), rl[t], ACT.Copy)

        send(0)
        k2_g = gathered("k2_g", dsc, k2_l, U8, "words")
        move_rows(nc.sync, k2_s, k2_g, range(4))
        send(1)
        k2_w = gathered("k2_w", dw, k2_l, U32, "stationary")
        b_ps = [ps.tile([P, 2 * S], F32, name=f"b{u}") for u in range(2)]
        for t in range(TILES):
            product(b_ps[t // 2][:, (t % 2) * S : (t % 2 + 1) * S], k2_w, k2_s, t, two_w[:], two_s[:])
        send(2)
        cand_g = gathered("cand_g", xsc, cand_l, U8, "bytes")
        move_rows(nc.sync, cand_s, cand_g, range(4))
        send(3)
        cand_w = gathered("cand_w", xw, cand_l, U32, "words")

        z = sb.tile([P, 2, PACK, S // 2], BF16, name="z", tag="stationary", align_bytes=64)
        for t in range(TILES):
            h_halves = h_ps[t][:].rearrange("p (u j) -> p u j", u=2)
            ds_halves = ds[t][:, :S].rearrange("p (u j) -> p u j", u=2)
            for us in [slice(0, 2)] if t < TILES - 1 else [slice(0, 1), slice(1, 2)]:
                nc.vector.scalar_tensor_tensor(
                    z[:, us, t, :], h_halves[:, us, :], g_neg[:, t : t + 1], ds_halves[:, us, :], ALU.mult, ALU.add
                )
        z_il = sb.tile([P, S * PACK], BF16, name="z_il", tag="z_diff", align_bytes=64)
        z_w = sb.tile([P, S], U32, name="z_w", align_bytes=64)
        z_s = sb.tile([P, S], U8, name="z_s", align_bytes=64)
        for u in range(2):
            nc.vector.tensor_copy(
                z_il[:, u * 2 * S : (u + 1) * 2 * S].rearrange("p (c i t) -> p c t i", i=4, t=PACK),
                z[:, u, :, :].rearrange("p t (c i) -> p c t i", i=4),
            )
        for u in range(2):
            half = slice(u * S // 2, (u + 1) * S // 2)
            nc.vector.quantize_mx(
                out=z_w[:, half].bitcast(FP8X4), scales=z_s[:, half], in_=z_il[:, u * 2 * S : (u + 1) * 2 * S]
            )
        a_ps = [ps.tile([P, 2 * S], F32, name=f"a{u}") for u in range(2)]
        for t in range(TILES):
            product(a_ps[t // 2][:, (t % 2) * S : (t % 2 + 1) * S], cand_w, cand_s, t, z_w[:], z_s[:])

        def cols(first, count):
            return slice(first * S, (first + count) * S)

        a_th = sb.tile([P, 2 * TILES * S], F32, name="a_th")
        b_got = sb.tile([P, TILES * S], F32, name="b_got")
        a_got = sb.tile([P, TILES * S], F32, name="a_got")
        diff = sb.tile([P, TILES * S], F32, name="diff", tag="z_diff", align_bytes=64)
        stay = sb.tile([P, TILES * S], F32, name="stay")
        come = sb.tile([P, TILES * S], F32, name="come")
        res = sb.tile([P, TILES * S], F32, name="res")
        out_rows = out.rearrange("(t p) j -> p t j", p=P)

        for u in range(2):
            nc.scalar.activation(b_rl[:, cols(2 * u, 2)], b_ps[u][:], ACT.Copy)
        for t in range(TILES):
            nc.scalar.activation(b_got[:, cols(t, 1)], b_rl[:, cols(t, 2)].indirect(n3_l[:]), ACT.Copy)
        for u in range(2):
            pair = cols(2 * u, 2)
            nc.vector.tensor_tensor(diff[:, pair], b_got[:, pair], b_rl[:, pair], ALU.subtract)
            nc.scalar.activation(a_th[:, cols(TILES + 2 * u, 2)], diff[:, pair], ACT.Tanh, scale=0.03125)
            nc.vector.tensor_scalar(a_th[:, pair], a_ps[u][:], 0.03125, None, ALU.mult)
        for t in range(TILES):
            nc.scalar.activation(a_got[:, cols(t, 1)], a_th[:, cols(t, 2)].indirect(n2_l[:]), ACT.Copy)

        def keep_part(u):
            nc.vector.scalar_tensor_tensor(
                stay[:, cols(2 * u, 2)], a_th[:, cols(TILES + 2 * u, 2)], 1.0, a_ps[u][:], ALU.subtract, ALU.mult
            )

        def fetched_part(first, count):
            span = cols(first, count)
            nc.vector.scalar_tensor_tensor(
                come[:, span], a_th[:, cols(TILES + first, count)], 1.0, a_got[:, span], ALU.add, ALU.mult
            )

        def finish(first, count):
            span = cols(first, count)
            nc.vector.scalar_tensor_tensor(res[:, span], stay[:, span], -0.03125, come[:, span], ALU.mult, ALU.add)
            nc.sync.dma_start(out_rows[:, first : first + count, :], res[:, span].rearrange("p (t j) -> p t j", j=S))

        keep_part(0)
        fetched_part(0, 2)
        keep_part(1)
        finish(0, 2)
        fetched_part(2, 1)
        fetched_part(3, 1)
        finish(2, 1)
        finish(3, 1)
